import numpy as np
import ml_dtypes


def mxq(x, axis, fmt="e4m3"):
    dtype, down = {"e4m3": (ml_dtypes.float8_e4m3fn, 7), "e5m2": (ml_dtypes.float8_e5m2, 14)}[fmt]
    v = np.moveaxis(np.asarray(x, np.float32).astype(ml_dtypes.bfloat16).astype(np.float64), axis, -1)
    blocks = v.reshape(v.shape[:-1] + (-1, 32))
    amax = np.abs(blocks).max(-1, keepdims=True)
    byte = np.maximum(np.where(amax > 0, np.frexp(amax)[1] - 1 + 127, 0) - down, 1)
    scale = np.exp2(byte - 127.0)
    codes = (blocks / scale).astype(np.float32).astype(dtype).astype(np.float64)
    return np.moveaxis((codes * scale).reshape(v.shape), -1, axis)


WIDE = False


def mx_kscale(k):
    if not WIDE:
        return np.ones(k)
    levels = np.array([10, -10, 5, -5, 0])
    if k % 512:
        return np.exp2(np.random.permutation(np.resize(levels, k // 32))).repeat(32)
    a = np.empty((k // 512, 16))
    for p in range(k // 512):
        a[p, :8] = np.random.permutation(np.resize(levels, 8))
        for g in range(8):
            far = levels[np.abs(levels - a[p, g]) >= 10]
            a[p, g + 8] = far[np.random.randint(len(far))]
    return np.exp2(a.ravel()).repeat(32)


def f64(x):
    return np.asarray(x).astype(np.float64)


E2M1 = np.array([0.0, 0.5, 1.0, 1.5, 2.0, 3.0, 4.0, 6.0, -0.0, -0.5, -1.0, -1.5, -2.0, -3.0, -4.0, -6.0])


def pack_weight(w, fmt):
    k, n = w.shape
    w = f64(np.asarray(w, np.float32).astype(ml_dtypes.bfloat16)).reshape(k // 32, 32, n)
    amax = np.abs(w).max(1)
    if fmt == "e4m3":
        byte = np.frexp(amax)[1] - 1 + 127 - 7
    else:
        mant, ex = np.frexp(amax / 6.0)
        byte = np.where(mant > 0.5, ex, ex - 1) + 127
    byte = np.clip(np.where(amax > 0, byte, 1), 1, 254)
    scaled = (w * np.exp2(127.0 - byte)[:, None, :]).reshape(k, n).astype(np.float32)
    by_word = np.ascontiguousarray(scaled.reshape(k // 512, 128, 4, n).transpose(0, 1, 3, 2))
    if fmt == "e4m3":
        words = by_word.astype(ml_dtypes.float8_e4m3fn).view(np.uint8)
    else:
        c = by_word.astype(ml_dtypes.float4_e2m1fn).view(np.uint8) & 0xF
        words = (c[..., 0::2] | (c[..., 1::2] << 4)).reshape(k // 512, 128, 2 * n)
    return np.ascontiguousarray(words), np.ascontiguousarray(byte.astype(np.uint8).reshape(k // 512, 16, n))


def unpack_weight(words, scales, fmt):
    g, _, n = scales.shape
    words = np.ascontiguousarray(words).reshape(g, 128, n, -1)
    if fmt == "e4m3":
        vals = words.view(ml_dtypes.float8_e4m3fn).astype(np.float64)
    else:
        nib = np.empty((g, 128, n, 4), np.uint8)
        nib[..., 0::2] = words & 0xF
        nib[..., 1::2] = words >> 4
        vals = E2M1[nib]
    vals = vals * np.repeat(np.exp2(scales.astype(np.float64) - 127.0), 8, axis=1)[..., None]
    return vals.transpose(0, 1, 3, 2).reshape(g * 512, n)


K, L, T, R, N = 1024, 512, 512, 512, 512


def setup_inputs():
    n = np.random.standard_normal
    fk = mx_kscale(K)
    fl = mx_kscale(L)
    fr = mx_kscale(R)
    xtp = pack_weight(n((K, T)) / fk[:, None], "e4m3")
    wap = pack_weight(n((K, R)) * 1 / np.sqrt(K) * fk[:, None], "e2m1")
    xqp = pack_weight(n((L, T)) / fl[:, None], "e4m3")
    wcp = pack_weight(n((L, R)) * 1 / np.sqrt(L) * fl[:, None], "e2m1")
    wbp = pack_weight(n((R, N)) * 1 / np.sqrt(R) / fr[:, None], "e4m3")
    wyp = pack_weight(n((K, N)) * 0.6 / np.sqrt(K) * fk[:, None], "e2m1")
    return {
        "xt_words": xtp[0],
        "xt_scales": xtp[1],
        "wa_words": wap[0],
        "wa_scales": wap[1],
        "xq_words": xqp[0],
        "xq_scales": xqp[1],
        "wc_words": wcp[0],
        "wc_scales": wcp[1],
        "us": (np.random.uniform(0.5, 2.0, (R, 1)) * fr[:, None]).astype(np.float32),
        "wb_words": wbp[0],
        "wb_scales": wbp[1],
        "wy_words": wyp[0],
        "wy_scales": wyp[1],
    }


def reference(xt_words, xt_scales, wa_words, wa_scales, xq_words, xq_scales, wc_words, wc_scales, us, wb_words, wb_scales, wy_words, wy_scales):
    xtu = unpack_weight(xt_words, xt_scales, "e4m3")
    wau = unpack_weight(wa_words, wa_scales, "e2m1")
    xqu = unpack_weight(xq_words, xq_scales, "e4m3")
    wcu = unpack_weight(wc_words, wc_scales, "e2m1")
    wbu = unpack_weight(wb_words, wb_scales, "e4m3")
    wyu = unpack_weight(wy_words, wy_scales, "e2m1")
    z = wau.T @ xtu + wcu.T @ xqu
    zp = np.pad(z, ((0, 0), (1, 0)))[:, :T]
    hid = z * np.tanh(zp) * f64(us)
    hidq = mxq(hid, 0, "e4m3")
    y = wbu.T @ hidq + wyu.T @ xtu
    return y

@@ -1,0 +1,191 @@
+from contextlib import ExitStack
+
+import concourse.mybir as mybir
+
+K, L, T, R, N = 1024, 512, 512, 512, 512
+FLOPS = 2 * T * (K * R + L * R + R * N + K * N)
+
+F32 = mybir.dt.float32
+BF16 = mybir.dt.bfloat16
+I32 = mybir.dt.int32
+U32 = mybir.dt.uint32
+U16 = mybir.dt.uint16
+U8 = mybir.dt.uint8
+E4M3X4 = mybir.dt.float8_e4m3fn_x4
+E2M1X4 = mybir.dt.float4_e2m1fn_x4
+ACT = mybir.ActivationFunctionType
+ALU = mybir.AluOpType
+
+P = 128
+PACK = 4
+COLS = 512
+HALF = T // 2
+PAD = 4
+STAGE0 = 16
+
+
+def tile_mix_hidden_pairs_multiplied_kernel(
+    tc, xt_words, xt_scales, wa_words, wa_scales, xq_words, xq_scales, wc_words, wc_scales,
+    us, wb_words, wb_scales, wy_words, wy_scales, out,
+):
+    nc = tc.nc
+    with ExitStack() as ctx:
+        sb = ctx.enter_context(tc.tile_pool(name="sb", bufs=1))
+        ps = ctx.enter_context(tc.psum_pool(name="ps", bufs=1))
+        ctx.enter_context(tc.manual_schedule())
+
+        def load_scale_rows(engine, stage, first, scales):
+            passes = scales.shape[0]
+            dst = stage[STAGE0 : STAGE0 + 16, first * COLS : (first + passes) * COLS].bitcast(I32)
+            engine.dma_start(
+                out=dst.rearrange("q (z c) -> q z c", z=passes),
+                in_=scales.rearrange("z q c -> q z c").bitcast(I32),
+            )
+
+        def spread_scale_rows(engine, planes, stage):
+            for q in range(4):
+                engine.dma_start(
+                    out=planes[32 * q : 32 * q + 4, :].bitcast(I32),
+                    in_=stage[STAGE0 + 4 * q : STAGE0 + 4 * q + 4, :].bitcast(I32),
+                )
+
+        def load_fp8(name, words):
+            codes = sb.tile([P, words.shape[0], COLS], U32, name=name, align_bytes=64)
+            nc.sync.dma_start(out=codes[:].bitcast(I32), in_=words.rearrange("z p c b -> p z (c b)").bitcast(I32))
+            return codes
+
+        def load_fp4(name, words):
+            codes = sb.tile([P, words.shape[0], 2 * COLS], U8, name=name, align_bytes=64)
+            nc.sync.dma_start(out=codes[:].bitcast(I32), in_=words.rearrange("z p c -> p z c").bitcast(I32))
+            return codes
+
+        stage1 = sb.tile([32, 6 * COLS], U8, align_bytes=64)
+        planes1 = sb.tile([P, 6 * COLS], U8, align_bytes=64)
+        stage2 = sb.tile([32, 3 * COLS], U8, align_bytes=64)
+        planes2 = sb.tile([P, 3 * COLS], U8, align_bytes=64)
+        us_sb = sb.tile([P, PACK], F32)
+        nc.gpsimd.dma_start(out=us_sb[:], in_=us.rearrange("(p j) o -> p (j o)", j=PACK))
+
+        load_scale_rows(nc.scalar, stage1, 0, wa_scales)
+        load_scale_rows(nc.scalar, stage1, 2, wc_scales)
+        load_scale_rows(nc.scalar, stage1, 3, xt_scales)
+        load_scale_rows(nc.scalar, stage1, 5, xq_scales)
+        wa = load_fp4("wa", wa_words)
+        wc = load_fp4("wc", wc_words)
+        xt = load_fp8("xt", xt_words)
+        xq = load_fp8("xq", xq_words)
+
+        nc.vector.memset(planes1[:].bitcast(U32), 0)
+        nc.vector.memset(planes2[:].bitcast(U32), 0)
+        th = []
+        for j in range(PACK):
+            th_j = sb.tile([P, PAD + T], F32, name="th%d" % j, align_bytes=64)
+            nc.vector.memset(th_j[:, PAD - 1 : PAD], 0.0)
+            th.append(th_j)
+
+        spread_scale_rows(nc.scalar, planes1, stage1)
+        warm = sb.tile([P, 1], F32)
+        nc.scalar.activation(out=warm[:], in_=th[0][:, PAD - 1 : PAD], func=ACT.Tanh)
+
+        load_scale_rows(nc.sync, stage2, 0, wy_scales)
+        load_scale_rows(nc.sync, stage2, 2, wb_scales)
+        wy = load_fp4("wy", wy_words)
+        wb = load_fp8("wb", wb_words)
+        spread_scale_rows(nc.sync, planes2, stage2)
+
+        wa_p = sb.tile([P, 2, 2 * COLS], U8, align_bytes=64)
+        wc_p = sb.tile([P, 1, 2 * COLS], U8, align_bytes=64)
+        for src, dst in ((wa, wa_p), (wc, wc_p)):
+            nc.vector.tensor_copy(
+                out=dst[:].bitcast(U16).rearrange("p z (j m) -> p z j m", j=PACK),
+                in_=src[:].bitcast(U16).rearrange("p z (m j) -> p z j m", j=PACK),
+            )
+        w_planes = planes1[:, 0 : 3 * COLS].rearrange("p (z m j) -> p j z m", z=3, j=PACK)
+        w_scale = []
+        for j in range(PACK):
+            ws_j = sb.tile([P, 3, P], U8, name="ws%d" % j, align_bytes=64)
+            nc.vector.tensor_copy(out=ws_j[:], in_=w_planes[:, j])
+            w_scale.append(ws_j)
+
+        first_layer = (
+            (wa_p, 0, xt, 0, 3),
+            (wa_p, 1, xt, 1, 4),
+            (wc_p, 0, xq, 0, 5),
+        )
+        pairs = sb.tile([P, 2, T, 2], BF16, align_bytes=64)
+        for j in range(PACK):
+            z = ps.tile([P, T], F32, name="z%d" % j)
+            for g, (w, wz, x, xz, plane) in enumerate(first_layer):
+                nc.tensor.matmul_mx(
+                    out=z[:],
+                    lhsT=w[:, wz, 2 * P * j : 2 * P * (j + 1)].bitcast(E2M1X4),
+                    lhsT_scale=w_scale[j][:, g, :],
+                    rhs=x[:, xz, :].bitcast(E4M3X4),
+                    rhs_scale=planes1[:, plane * COLS : (plane + 1) * COLS],
+                    start=(g == 0),
+                    stop=(g == 2),
+                )
+            nc.scalar.activation(out=th[j][:, PAD : PAD + T - 1], in_=z[:, 0 : T - 1], func=ACT.Tanh)
+            spans = ((0, T),) if j < PACK - 1 else ((0, HALF), (HALF, T))
+            for t0, t1 in spans:
+                nc.vector.scalar_tensor_tensor(
+                    out=pairs[:, j // 2, t0:t1, j % 2],
+                    in0=z[:, t0:t1],
+                    scalar=us_sb[:, j : j + 1],
+                    in1=th[j][:, PAD - 1 + t0 : PAD - 1 + t1],
+                    op0=ALU.mult,
+                    op1=ALU.mult,
+                )
+
+        acc = []
+        for i in range(4):
+            acc_i = ps.tile([P, T], F32, name="acc%d" % i)
+            for g in range(2):
+                nc.tensor.matmul_mx(
+                    out=acc_i[:],
+                    lhsT=wy[:, g, 2 * P * i : 2 * P * (i + 1)].bitcast(E2M1X4),
+                    lhsT_scale=planes2[:, g * COLS + P * i : g * COLS + P * (i + 1)],
+                    rhs=xt[:, g, :].bitcast(E4M3X4),
+                    rhs_scale=planes1[:, (3 + g) * COLS : (4 + g) * COLS],
+                    start=(g == 0),
+                    stop=False,
+                )
+            acc.append(acc_i)
+
+        pair_words = pairs[:].rearrange("p u t e -> p u (t e)").bitcast(F32).rearrange("p u t -> p t u")
+        hid = []
+        for h in range(2):
+            hid_h = sb.tile([P, HALF, 2], F32, name="hid%d" % h, align_bytes=64)
+            nc.vector.tensor_copy(out=hid_h[:], in_=pair_words[:, h * HALF : (h + 1) * HALF, :])
+            hid.append(hid_h)
+        hid_codes = []
+        hid_scales = []
+        for h in range(2):
+            codes_h = sb.tile([P, HALF], U32, name="hc%d" % h, align_bytes=64)
+            scales_h = sb.tile([P, HALF], U8, name="hs%d" % h, align_bytes=64)
+            nc.vector.quantize_mx(
+                out=codes_h[:].bitcast(E4M3X4),
+                scales=scales_h[:],
+                in_=hid[h][:].rearrange("p t u -> p (t u)").bitcast(BF16),
+            )
+            hid_codes.append(codes_h)
+            hid_scales.append(scales_h)
+
+        for h in range(2):
+            for i in range(4):
+                nc.tensor.matmul_mx(
+                    out=acc[i][:, h * HALF : (h + 1) * HALF],
+                    lhsT=wb[:, 0, P * i : P * (i + 1)].bitcast(E4M3X4),
+                    lhsT_scale=planes2[:, 2 * COLS + P * i : 2 * COLS + P * (i + 1)],
+                    rhs=hid_codes[h][:].bitcast(E4M3X4),
+                    rhs_scale=hid_scales[h][:],
+                    start=False,
+                    stop=(h == 1),
+                )
+        for i in range(4):
+            res = sb.tile([P, T], F32, name="res%d" % i)
+            if i % 2 == 0:
+                nc.scalar.copy(out=res[:], in_=acc[i][:])
+            else:
+                nc.vector.tensor_copy(out=res[:], in_=acc[i][:])
+            nc.sync.dma_start(out=out[P * i : P * (i + 1), :], in_=res[:])

@@ -22,6 +22,8 @@ COLS = 512
 HALF = T // 2
 PAD = 4
 STAGE0 = 16
+WARM_FREE = 18
+WARM_XT = 8
 
 
 def tile_mix_hidden_pairs_multiplied_kernel(
@@ -42,21 +44,21 @@ def tile_mix_hidden_pairs_multiplied_kernel(
                 in_=scales.rearrange("z q c -> q z c").bitcast(I32),
             )
 
-        def spread_scale_rows(engine, planes, stage):
+        def spread_scale_rows(engines, planes, stage):
             for q in range(4):
-                engine.dma_start(
+                engines[q % 2].dma_start(
                     out=planes[32 * q : 32 * q + 4, :].bitcast(I32),
                     in_=stage[STAGE0 + 4 * q : STAGE0 + 4 * q + 4, :].bitcast(I32),
                 )
 
-        def load_fp8(name, words):
+        def load_fp8(engine, name, words):
             codes = sb.tile([P, words.shape[0], COLS], U32, name=name, align_bytes=64)
-            nc.sync.dma_start(out=codes[:].bitcast(I32), in_=words.rearrange("z p c b -> p z (c b)").bitcast(I32))
+            engine.dma_start(out=codes[:].bitcast(I32), in_=words.rearrange("z p c b -> p z (c b)").bitcast(I32))
             return codes
 
-        def load_fp4(name, words):
+        def load_fp4(engine, name, words):
             codes = sb.tile([P, words.shape[0], 2 * COLS], U8, name=name, align_bytes=64)
-            nc.sync.dma_start(out=codes[:].bitcast(I32), in_=words.rearrange("z p c -> p z c").bitcast(I32))
+            engine.dma_start(out=codes[:].bitcast(I32), in_=words.rearrange("z p c -> p z c").bitcast(I32))
             return codes
 
         stage1 = sb.tile([32, 6 * COLS], U8, align_bytes=64)
@@ -64,34 +66,53 @@ def tile_mix_hidden_pairs_multiplied_kernel(
         stage2 = sb.tile([32, 3 * COLS], U8, align_bytes=64)
         planes2 = sb.tile([P, 3 * COLS], U8, align_bytes=64)
         us_sb = sb.tile([P, PACK], F32)
-        nc.gpsimd.dma_start(out=us_sb[:], in_=us.rearrange("(p j) o -> p (j o)", j=PACK))
 
-        load_scale_rows(nc.scalar, stage1, 0, wa_scales)
+        load_scale_rows(nc.sync, stage1, 0, wa_scales)
         load_scale_rows(nc.scalar, stage1, 2, wc_scales)
-        load_scale_rows(nc.scalar, stage1, 3, xt_scales)
+        load_scale_rows(nc.sync, stage1, 3, xt_scales)
         load_scale_rows(nc.scalar, stage1, 5, xq_scales)
-        wa = load_fp4("wa", wa_words)
-        wc = load_fp4("wc", wc_words)
-        xt = load_fp8("xt", xt_words)
-        xq = load_fp8("xq", xq_words)
+        wa = load_fp4(nc.sync, "wa", wa_words)
+        wc = load_fp4(nc.scalar, "wc", wc_words)
+        xt = load_fp8(nc.sync, "xt", xt_words)
+        xq = load_fp8(nc.scalar, "xq", xq_words)
 
-        nc.vector.memset(planes1[:].bitcast(U32), 0)
-        nc.vector.memset(planes2[:].bitcast(U32), 0)
+        zeros = sb.tile([P, PACK * P], BF16, align_bytes=64)
+        zero_codes = sb.tile([P, P], U32, align_bytes=64)
+        zero_scales = sb.tile([P, P], U8, align_bytes=64)
+        nc.vector.memset(zeros[:], 0.0)
         th = []
         for j in range(PACK):
             th_j = sb.tile([P, PAD + T], F32, name="th%d" % j, align_bytes=64)
             nc.vector.memset(th_j[:, PAD - 1 : PAD], 0.0)
             th.append(th_j)
+        nc.vector.quantize_mx(out=zero_codes[:].bitcast(E4M3X4), scales=zero_scales[:], in_=zeros[:])
+        nc.vector.memset(planes1[:].bitcast(U32), 0)
+        nc.vector.memset(planes2[:].bitcast(U32), 0)
 
-        spread_scale_rows(nc.scalar, planes1, stage1)
+        acc = []
+        for i in range(4):
+            acc_i = ps.tile([P, T], F32, name="acc%d" % i)
+            acc.append(acc_i)
+        for w in range(WARM_FREE + WARM_XT):
+            nc.tensor.matmul_mx(
+                out=acc[3][:, 0:P],
+                lhsT=(zero_codes[:] if w < WARM_FREE else xt[:, 0, 0:P]).bitcast(E4M3X4),
+                lhsT_scale=zero_scales[:],
+                rhs=zero_codes[:].bitcast(E4M3X4),
+                rhs_scale=zero_scales[:],
+                start=True,
+                stop=True,
+            )
+
+        spread_scale_rows((nc.sync, nc.scalar), planes1, stage1)
         warm = sb.tile([P, 1], F32)
         nc.scalar.activation(out=warm[:], in_=th[0][:, PAD - 1 : PAD], func=ACT.Tanh)
-
+        nc.sync.dma_start(out=us_sb[:], in_=us.rearrange("(p j) o -> p (j o)", j=PACK))
         load_scale_rows(nc.sync, stage2, 0, wy_scales)
         load_scale_rows(nc.sync, stage2, 2, wb_scales)
-        wy = load_fp4("wy", wy_words)
-        wb = load_fp8("wb", wb_words)
-        spread_scale_rows(nc.sync, planes2, stage2)
+        wy = load_fp4(nc.sync, "wy", wy_words)
+        wb = load_fp8(nc.sync, "wb", wb_words)
+        spread_scale_rows((nc.sync, nc.sync), planes2, stage2)
 
         wa_p = sb.tile([P, 2, 2 * COLS], U8, align_bytes=64)
         wc_p = sb.tile([P, 1, 2 * COLS], U8, align_bytes=64)
@@ -137,12 +158,10 @@ def tile_mix_hidden_pairs_multiplied_kernel(
                     op1=ALU.mult,
                 )
 
-        acc = []
         for i in range(4):
-            acc_i = ps.tile([P, T], F32, name="acc%d" % i)
             for g in range(2):
                 nc.tensor.matmul_mx(
-                    out=acc_i[:],
+                    out=acc[i][:],
                     lhsT=wy[:, g, 2 * P * i : 2 * P * (i + 1)].bitcast(E2M1X4),
                     lhsT_scale=planes2[:, g * COLS + P * i : g * COLS + P * (i + 1)],
                     rhs=xt[:, g, :].bitcast(E4M3X4),
@@ -150,7 +169,6 @@ def tile_mix_hidden_pairs_multiplied_kernel(
                     start=(g == 0),
                     stop=False,
                 )
-            acc.append(acc_i)
 
         pair_words = pairs[:].rearrange("p u t e -> p u (t e)").bitcast(F32).rearrange("p u t -> p t u")
         hid = []
@@ -171,8 +189,8 @@ def tile_mix_hidden_pairs_multiplied_kernel(
             hid_codes.append(codes_h)
             hid_scales.append(scales_h)
 
-        for h in range(2):
-            for i in range(4):
+        for h, i in ((0, 0), (0, 1), (1, 0), (1, 1), (0, 2), (1, 2), (0, 3), (1, 3)):
+            if True:
                 nc.tensor.matmul_mx(
                     out=acc[i][:, h * HALF : (h + 1) * HALF],
                     lhsT=wb[:, 0, P * i : P * (i + 1)].bitcast(E4M3X4),

@@ -71,10 +71,10 @@ def tile_mix_hidden_pairs_multiplied_kernel(
         load_scale_rows(nc.scalar, stage1, 2, wc_scales)
         load_scale_rows(nc.sync, stage1, 3, xt_scales)
         load_scale_rows(nc.scalar, stage1, 5, xq_scales)
+        load_scale_rows(nc.sync, stage2, 0, wy_scales)
+        load_scale_rows(nc.scalar, stage2, 2, wb_scales)
         wa = load_fp4(nc.sync, "wa", wa_words)
-        wc = load_fp4(nc.scalar, "wc", wc_words)
-        xt = load_fp8(nc.sync, "xt", xt_words)
-        xq = load_fp8(nc.scalar, "xq", xq_words)
+        xt = load_fp8(nc.scalar, "xt", xt_words)
 
         zeros = sb.tile([P, PACK * P], BF16, align_bytes=64)
         zero_codes = sb.tile([P, P], U32, align_bytes=64)
@@ -90,12 +90,12 @@ def tile_mix_hidden_pairs_multiplied_kernel(
         nc.vector.memset(planes2[:].bitcast(U32), 0)
 
         acc = []
-        for i in range(4):
-            acc_i = ps.tile([P, T], F32, name="acc%d" % i)
+        for i in range(2):
+            acc_i = ps.tile([P, HALF], F32, name="acc%d" % i)
             acc.append(acc_i)
         for w in range(WARM_FREE + WARM_XT):
             nc.tensor.matmul_mx(
-                out=acc[3][:, 0:P],
+                out=acc[1][:, 0:P],
                 lhsT=(zero_codes[:] if w < WARM_FREE else xt[:, 0, 0:P]).bitcast(E4M3X4),
                 lhsT_scale=zero_scales[:],
                 rhs=zero_codes[:].bitcast(E4M3X4),
@@ -105,105 +105,159 @@ def tile_mix_hidden_pairs_multiplied_kernel(
             )
 
         spread_scale_rows((nc.sync, nc.scalar), planes1, stage1)
+        wc = load_fp4(nc.sync, "wc", wc_words)
+        xq = load_fp8(nc.scalar, "xq", xq_words)
         warm = sb.tile([P, 1], F32)
         nc.scalar.activation(out=warm[:], in_=th[0][:, PAD - 1 : PAD], func=ACT.Tanh)
         nc.sync.dma_start(out=us_sb[:], in_=us.rearrange("(p j) o -> p (j o)", j=PACK))
-        load_scale_rows(nc.sync, stage2, 0, wy_scales)
-        load_scale_rows(nc.sync, stage2, 2, wb_scales)
         wy = load_fp4(nc.sync, "wy", wy_words)
-        wb = load_fp8(nc.sync, "wb", wb_words)
         spread_scale_rows((nc.sync, nc.sync), planes2, stage2)
+        wb = load_fp8(nc.sync, "wb", wb_words)
 
         wa_p = sb.tile([P, 2, 2 * COLS], U8, align_bytes=64)
         wc_p = sb.tile([P, 1, 2 * COLS], U8, align_bytes=64)
-        for src, dst in ((wa, wa_p), (wc, wc_p)):
+
+        def permute_codes(dst, src):
             nc.vector.tensor_copy(
                 out=dst[:].bitcast(U16).rearrange("p z (j m) -> p z j m", j=PACK),
                 in_=src[:].bitcast(U16).rearrange("p z (m j) -> p z j m", j=PACK),
             )
+
         w_planes = planes1[:, 0 : 3 * COLS].rearrange("p (z m j) -> p j z m", z=3, j=PACK)
+        permute_codes(wa_p, wa)
         w_scale = []
-        for j in range(PACK):
+        first_scales = []
+        for g in range(3):
+            ws_g = sb.tile([P, P], U8, name="ws0%d" % g, align_bytes=64)
+            if g == 2:
+                permute_codes(wc_p, wc)
+            nc.vector.tensor_copy(out=ws_g[:], in_=w_planes[:, 0, g])
+            first_scales.append(ws_g[:])
+        w_scale.append(first_scales)
+        for j in range(1, PACK):
             ws_j = sb.tile([P, 3, P], U8, name="ws%d" % j, align_bytes=64)
             nc.vector.tensor_copy(out=ws_j[:], in_=w_planes[:, j])
-            w_scale.append(ws_j)
+            w_scale.append([ws_j[:, g, :] for g in range(3)])
 
         first_layer = (
             (wa_p, 0, xt, 0, 3),
             (wa_p, 1, xt, 1, 4),
             (wc_p, 0, xq, 0, 5),
         )
-        pairs = sb.tile([P, 2, T, 2], BF16, align_bytes=64)
-        for j in range(PACK):
-            z = ps.tile([P, T], F32, name="z%d" % j)
-            for g, (w, wz, x, xz, plane) in enumerate(first_layer):
-                nc.tensor.matmul_mx(
-                    out=z[:],
-                    lhsT=w[:, wz, 2 * P * j : 2 * P * (j + 1)].bitcast(E2M1X4),
-                    lhsT_scale=w_scale[j][:, g, :],
-                    rhs=x[:, xz, :].bitcast(E4M3X4),
-                    rhs_scale=planes1[:, plane * COLS : (plane + 1) * COLS],
-                    start=(g == 0),
-                    stop=(g == 2),
-                )
-            nc.scalar.activation(out=th[j][:, PAD : PAD + T - 1], in_=z[:, 0 : T - 1], func=ACT.Tanh)
-            spans = ((0, T),) if j < PACK - 1 else ((0, HALF), (HALF, T))
-            for t0, t1 in spans:
-                nc.vector.scalar_tensor_tensor(
-                    out=pairs[:, j // 2, t0:t1, j % 2],
-                    in0=z[:, t0:t1],
-                    scalar=us_sb[:, j : j + 1],
-                    in1=th[j][:, PAD - 1 + t0 : PAD - 1 + t1],
-                    op0=ALU.mult,
-                    op1=ALU.mult,
-                )
-
-        for i in range(4):
-            for g in range(2):
-                nc.tensor.matmul_mx(
-                    out=acc[i][:],
-                    lhsT=wy[:, g, 2 * P * i : 2 * P * (i + 1)].bitcast(E2M1X4),
-                    lhsT_scale=planes2[:, g * COLS + P * i : g * COLS + P * (i + 1)],
-                    rhs=xt[:, g, :].bitcast(E4M3X4),
-                    rhs_scale=planes1[:, (3 + g) * COLS : (4 + g) * COLS],
-                    start=(g == 0),
-                    stop=False,
-                )
-
-        pair_words = pairs[:].rearrange("p u t e -> p u (t e)").bitcast(F32).rearrange("p u t -> p t u")
-        hid = []
+        pairs = []
         for h in range(2):
-            hid_h = sb.tile([P, HALF, 2], F32, name="hid%d" % h, align_bytes=64)
-            nc.vector.tensor_copy(out=hid_h[:], in_=pair_words[:, h * HALF : (h + 1) * HALF, :])
-            hid.append(hid_h)
+            pairs_h = sb.tile([P, 2, HALF, 2], BF16, name="pairs%d" % h, align_bytes=64)
+            pairs.append(pairs_h)
+        hid = []
         hid_codes = []
         hid_scales = []
         for h in range(2):
+            hid_h = sb.tile([P, HALF, 2], F32, name="hid%d" % h, align_bytes=64)
             codes_h = sb.tile([P, HALF], U32, name="hc%d" % h, align_bytes=64)
             scales_h = sb.tile([P, HALF], U8, name="hs%d" % h, align_bytes=64)
-            nc.vector.quantize_mx(
-                out=codes_h[:].bitcast(E4M3X4),
-                scales=scales_h[:],
-                in_=hid[h][:].rearrange("p t u -> p (t u)").bitcast(BF16),
-            )
+            hid.append(hid_h)
             hid_codes.append(codes_h)
             hid_scales.append(scales_h)
 
-        for h, i in ((0, 0), (0, 1), (1, 0), (1, 1), (0, 2), (1, 2), (0, 3), (1, 3)):
-            if True:
-                nc.tensor.matmul_mx(
-                    out=acc[i][:, h * HALF : (h + 1) * HALF],
-                    lhsT=wb[:, 0, P * i : P * (i + 1)].bitcast(E4M3X4),
-                    lhsT_scale=planes2[:, 2 * COLS + P * i : 2 * COLS + P * (i + 1)],
-                    rhs=hid_codes[h][:].bitcast(E4M3X4),
-                    rhs_scale=hid_scales[h][:],
-                    start=False,
-                    stop=(h == 1),
-                )
+        z_halves = {}
+
+        def first_layer_passes(z, j, t0, width, step):
+            for c in range(0, width, step):
+                for g, (w, wz, x, xz, plane) in enumerate(first_layer):
+                    nc.tensor.matmul_mx(
+                        out=z[:, c : c + step],
+                        lhsT=w[:, wz, 2 * P * j : 2 * P * (j + 1)].bitcast(E2M1X4),
+                        lhsT_scale=w_scale[j][g],
+                        rhs=x[:, xz, t0 + c : t0 + c + step].bitcast(E4M3X4),
+                        rhs_scale=planes1[:, plane * COLS + t0 + c : plane * COLS + t0 + c + step],
+                        start=(c == 0 and g == 0),
+                        stop=(c + step == width and g == 2),
+                    )
+            n_tanh = min(width, T - 1 - t0)
+            nc.scalar.activation(out=th[j][:, PAD + t0 : PAD + t0 + n_tanh], in_=z[:, 0:n_tanh], func=ACT.Tanh)
+
+        def product(j, h):
+            t0 = h * HALF
+            nc.vector.scalar_tensor_tensor(
+                out=pairs[h][:, j // 2, :, j % 2],
+                in0=z_halves[j, h],
+                scalar=us_sb[:, j : j + 1],
+                in1=th[j][:, PAD - 1 + t0 : PAD - 1 + t0 + HALF],
+                op0=ALU.mult,
+                op1=ALU.mult,
+            )
+
+        def merge(h):
+            pair_words = pairs[h][:].rearrange("p u t e -> p u (t e)").bitcast(F32)
+            nc.scalar.copy(out=hid[h][:], in_=pair_words.rearrange("p u t -> p t u"))
+
+        def quantise(h):
+            nc.vector.quantize_mx(
+                out=hid_codes[h][:].bitcast(E4M3X4),
+                scales=hid_scales[h][:],
+                in_=hid[h][:].rearrange("p t u -> p (t u)").bitcast(BF16),
+            )
+
+        for j in range(2):
+            z = ps.tile([P, T], F32, name="z%d" % j, tag="z%d" % j)
+            first_layer_passes(z, j, 0, T, T)
+            for h in range(2):
+                z_halves[j, h] = z[:, h * HALF : (h + 1) * HALF]
+        for h in range(2):
+            for j in range(2, PACK):
+                z = ps.tile([P, HALF], F32, name="z%d%d" % (j, h), tag="z%d%d" % (j, h))
+                first_layer_passes(z, j, h * HALF, HALF, P)
+                z_halves[j, h] = z[:]
+
+        for j, h in ((0, 0), (0, 1), (1, 0), (2, 0), (3, 0), (1, 1), (2, 1), (3, 1)):
+            product(j, h)
+        for h in range(2):
+            merge(h)
+            quantise(h)
+
+        for tag in ("z0", "z20", "z30", "z1", "z21", "z31"):
+            acc_i = ps.tile([P, HALF], F32, name="acc_" + tag, tag=tag)
+            acc.append(acc_i)
+
+        def skip_passes(h, i):
+            for g in range(2):
+                for c in range(2):
+                    t0 = h * HALF + c * P
+                    nc.tensor.matmul_mx(
+                        out=acc[4 * h + i][:, c * P : (c + 1) * P],
+                        lhsT=wy[:, g, 2 * P * i : 2 * P * (i + 1)].bitcast(E2M1X4),
+                        lhsT_scale=planes2[:, g * COLS + P * i : g * COLS + P * (i + 1)],
+                        rhs=xt[:, g, t0 : t0 + P].bitcast(E4M3X4),
+                        rhs_scale=planes1[:, (3 + g) * COLS + t0 : (3 + g) * COLS + t0 + P],
+                        start=(c == 0 and g == 0),
+                        stop=False,
+                    )
+
+        def hidden_pass(h, i):
+            nc.tensor.matmul_mx(
+                out=acc[4 * h + i][:],
+                lhsT=wb[:, 0, P * i : P * (i + 1)].bitcast(E4M3X4),
+                lhsT_scale=planes2[:, 2 * COLS + P * i : 2 * COLS + P * (i + 1)],
+                rhs=hid_codes[h][:].bitcast(E4M3X4),
+                rhs_scale=hid_scales[h][:],
+                start=False,
+                stop=True,
+            )
+
         for i in range(4):
-            res = sb.tile([P, T], F32, name="res%d" % i)
-            if i % 2 == 0:
-                nc.scalar.copy(out=res[:], in_=acc[i][:])
-            else:
-                nc.vector.tensor_copy(out=res[:], in_=acc[i][:])
-            nc.sync.dma_start(out=out[P * i : P * (i + 1), :], in_=res[:])
+            skip_passes(0, i)
+        for i in range(3):
+            skip_passes(1, i)
+        for i in range(4):
+            hidden_pass(0, i)
+        skip_passes(1, 3)
+        for i in range(4):
+            hidden_pass(1, i)
+        for h in range(2):
+            for i in range(4):
+                res = sb.tile([P, HALF], F32, name="res%d%d" % (h, i))
+                if h == 1 and i % 2 == 0:
+                    nc.vector.tensor_copy(out=res[:], in_=acc[4 * h + i][:])
+                else:
+                    nc.scalar.copy(out=res[:], in_=acc[4 * h + i][:])
+                nc.sync.dma_start(out=out[P * i : P * (i + 1), h * HALF : (h + 1) * HALF], in_=res[:])

@@ -20,10 +20,17 @@ P = 128
 PACK = 4
 COLS = 512
 HALF = T // 2
+N_TILES = N // P
+SCALE_ROWS = 16
+QUADRANT = 32
+STAGE_ROW = 16
 PAD = 4
-STAGE0 = 16
-WARM_FREE = 18
-WARM_XT = 8
+WHOLE_TILES = 2
+WARM_AT_START = 18
+WARM_AFTER_XT = 12
+
+WA_AT, WC_AT, XT_AT, XQ_AT, FIRST_PASSES = 0, 2, 3, 5, 6
+WY_AT, WB_AT, SECOND_PASSES = 0, 2, 3
 
 
 def tile_mix_hidden_pairs_multiplied_kernel(
@@ -36,19 +43,19 @@ def tile_mix_hidden_pairs_multiplied_kernel(
         ps = ctx.enter_context(tc.psum_pool(name="ps", bufs=1))
         ctx.enter_context(tc.manual_schedule())
 
-        def load_scale_rows(engine, stage, first, scales):
+        def stage_scale_rows(engine, stage, at, scales):
             passes = scales.shape[0]
-            dst = stage[STAGE0 : STAGE0 + 16, first * COLS : (first + passes) * COLS].bitcast(I32)
+            rows = stage[STAGE_ROW : STAGE_ROW + SCALE_ROWS, at * COLS : (at + passes) * COLS].bitcast(I32)
             engine.dma_start(
-                out=dst.rearrange("q (z c) -> q z c", z=passes),
+                out=rows.rearrange("q (z c) -> q z c", z=passes),
                 in_=scales.rearrange("z q c -> q z c").bitcast(I32),
             )
 
         def spread_scale_rows(engines, planes, stage):
-            for q in range(4):
-                engines[q % 2].dma_start(
-                    out=planes[32 * q : 32 * q + 4, :].bitcast(I32),
-                    in_=stage[STAGE0 + 4 * q : STAGE0 + 4 * q + 4, :].bitcast(I32),
+            for s in range(4):
+                engines[s % len(engines)].dma_start(
+                    out=planes[s:P:QUADRANT, :].bitcast(I32),
+                    in_=stage[STAGE_ROW + s : STAGE_ROW + SCALE_ROWS : 4, :].bitcast(I32),
                 )
 
         def load_fp8(engine, name, words):
@@ -61,18 +68,18 @@ def tile_mix_hidden_pairs_multiplied_kernel(
             engine.dma_start(out=codes[:].bitcast(I32), in_=words.rearrange("z p c -> p z c").bitcast(I32))
             return codes
 
-        stage1 = sb.tile([32, 6 * COLS], U8, align_bytes=64)
-        planes1 = sb.tile([P, 6 * COLS], U8, align_bytes=64)
-        stage2 = sb.tile([32, 3 * COLS], U8, align_bytes=64)
-        planes2 = sb.tile([P, 3 * COLS], U8, align_bytes=64)
+        stage1 = sb.tile([STAGE_ROW + SCALE_ROWS, FIRST_PASSES * COLS], U8, align_bytes=64)
+        planes1 = sb.tile([P, FIRST_PASSES * COLS], U8, align_bytes=64)
+        stage2 = sb.tile([STAGE_ROW + SCALE_ROWS, SECOND_PASSES * COLS], U8, align_bytes=64)
+        planes2 = sb.tile([P, SECOND_PASSES * COLS], U8, align_bytes=64)
         us_sb = sb.tile([P, PACK], F32)
 
-        load_scale_rows(nc.sync, stage1, 0, wa_scales)
-        load_scale_rows(nc.scalar, stage1, 2, wc_scales)
-        load_scale_rows(nc.sync, stage1, 3, xt_scales)
-        load_scale_rows(nc.scalar, stage1, 5, xq_scales)
-        load_scale_rows(nc.sync, stage2, 0, wy_scales)
-        load_scale_rows(nc.scalar, stage2, 2, wb_scales)
+        stage_scale_rows(nc.sync, stage1, WA_AT, wa_scales)
+        stage_scale_rows(nc.scalar, stage1, WC_AT, wc_scales)
+        stage_scale_rows(nc.sync, stage1, XT_AT, xt_scales)
+        stage_scale_rows(nc.scalar, stage1, XQ_AT, xq_scales)
+        stage_scale_rows(nc.sync, stage2, WY_AT, wy_scales)
+        stage_scale_rows(nc.scalar, stage2, WB_AT, wb_scales)
         wa = load_fp4(nc.sync, "wa", wa_words)
         xt = load_fp8(nc.scalar, "xt", xt_words)
 
@@ -80,11 +87,11 @@ def tile_mix_hidden_pairs_multiplied_kernel(
         zero_codes = sb.tile([P, P], U32, align_bytes=64)
         zero_scales = sb.tile([P, P], U8, align_bytes=64)
         nc.vector.memset(zeros[:], 0.0)
-        th = []
+        tanh_z = []
         for j in range(PACK):
-            th_j = sb.tile([P, PAD + T], F32, name="th%d" % j, align_bytes=64)
-            nc.vector.memset(th_j[:, PAD - 1 : PAD], 0.0)
-            th.append(th_j)
+            tanh_j = sb.tile([P, PAD + T], F32, name="tanh%d" % j, align_bytes=64)
+            nc.vector.memset(tanh_j[:, PAD - 1 : PAD], 0.0)
+            tanh_z.append(tanh_j)
         nc.vector.quantize_mx(out=zero_codes[:].bitcast(E4M3X4), scales=zero_scales[:], in_=zeros[:])
         nc.vector.memset(planes1[:].bitcast(U32), 0)
         nc.vector.memset(planes2[:].bitcast(U32), 0)
@@ -93,10 +100,11 @@ def tile_mix_hidden_pairs_multiplied_kernel(
         for i in range(2):
             acc_i = ps.tile([P, HALF], F32, name="acc%d" % i)
             acc.append(acc_i)
-        for w in range(WARM_FREE + WARM_XT):
+
+        for w in range(WARM_AT_START + WARM_AFTER_XT):
             nc.tensor.matmul_mx(
                 out=acc[1][:, 0:P],
-                lhsT=(zero_codes[:] if w < WARM_FREE else xt[:, 0, 0:P]).bitcast(E4M3X4),
+                lhsT=(zero_codes[:] if w < WARM_AT_START else xt[:, 0, 0:P]).bitcast(E4M3X4),
                 lhsT_scale=zero_scales[:],
                 rhs=zero_codes[:].bitcast(E4M3X4),
                 rhs_scale=zero_scales[:],
@@ -107,113 +115,105 @@ def tile_mix_hidden_pairs_multiplied_kernel(
         spread_scale_rows((nc.sync, nc.scalar), planes1, stage1)
         wc = load_fp4(nc.sync, "wc", wc_words)
         xq = load_fp8(nc.scalar, "xq", xq_words)
-        warm = sb.tile([P, 1], F32)
-        nc.scalar.activation(out=warm[:], in_=th[0][:, PAD - 1 : PAD], func=ACT.Tanh)
+        table_warm = sb.tile([P, 1], F32)
+        nc.scalar.activation(out=table_warm[:], in_=tanh_z[0][:, PAD - 1 : PAD], func=ACT.Tanh)
         nc.sync.dma_start(out=us_sb[:], in_=us.rearrange("(p j) o -> p (j o)", j=PACK))
         wy = load_fp4(nc.sync, "wy", wy_words)
-        spread_scale_rows((nc.sync, nc.sync), planes2, stage2)
+        spread_scale_rows((nc.sync,), planes2, stage2)
         wb = load_fp8(nc.sync, "wb", wb_words)
 
-        wa_p = sb.tile([P, 2, 2 * COLS], U8, align_bytes=64)
-        wc_p = sb.tile([P, 1, 2 * COLS], U8, align_bytes=64)
+        wa_by_tile = sb.tile([P, 2, 2 * COLS], U8, align_bytes=64)
+        wc_by_tile = sb.tile([P, 1, 2 * COLS], U8, align_bytes=64)
 
-        def permute_codes(dst, src):
+        def permute_words(dst, src):
             nc.vector.tensor_copy(
                 out=dst[:].bitcast(U16).rearrange("p z (j m) -> p z j m", j=PACK),
                 in_=src[:].bitcast(U16).rearrange("p z (m j) -> p z j m", j=PACK),
             )
 
-        w_planes = planes1[:, 0 : 3 * COLS].rearrange("p (z m j) -> p j z m", z=3, j=PACK)
-        permute_codes(wa_p, wa)
-        w_scale = []
-        first_scales = []
-        for g in range(3):
-            ws_g = sb.tile([P, P], U8, name="ws0%d" % g, align_bytes=64)
-            if g == 2:
-                permute_codes(wc_p, wc)
-            nc.vector.tensor_copy(out=ws_g[:], in_=w_planes[:, 0, g])
-            first_scales.append(ws_g[:])
-        w_scale.append(first_scales)
-        for j in range(1, PACK):
-            ws_j = sb.tile([P, 3, P], U8, name="ws%d" % j, align_bytes=64)
-            nc.vector.tensor_copy(out=ws_j[:], in_=w_planes[:, j])
-            w_scale.append([ws_j[:, g, :] for g in range(3)])
-
         first_layer = (
-            (wa_p, 0, xt, 0, 3),
-            (wa_p, 1, xt, 1, 4),
-            (wc_p, 0, xq, 0, 5),
+            (wa_by_tile, 0, xt, 0, XT_AT),
+            (wa_by_tile, 1, xt, 1, XT_AT + 1),
+            (wc_by_tile, 0, xq, 0, XQ_AT),
         )
+        n_first = len(first_layer)
+        weight_planes = planes1[:, 0 : n_first * COLS].rearrange("p (g m j) -> p j g m", g=n_first, j=PACK)
+
+        permute_words(wa_by_tile, wa)
+        tile0_scales = []
+        for g in range(n_first):
+            scales_g = sb.tile([P, P], U8, name="w_scales0%d" % g, align_bytes=64)
+            if g == WC_AT:
+                permute_words(wc_by_tile, wc)
+            nc.vector.tensor_copy(out=scales_g[:], in_=weight_planes[:, 0, g])
+            tile0_scales.append(scales_g[:])
+        w_scales = [tile0_scales]
+        for j in range(1, PACK):
+            scales_j = sb.tile([P, n_first, P], U8, name="w_scales%d" % j, align_bytes=64)
+            nc.vector.tensor_copy(out=scales_j[:], in_=weight_planes[:, j])
+            w_scales.append([scales_j[:, g, :] for g in range(n_first)])
+
         pairs = []
         for h in range(2):
             pairs_h = sb.tile([P, 2, HALF, 2], BF16, name="pairs%d" % h, align_bytes=64)
             pairs.append(pairs_h)
-        hid = []
+        hid_words = []
         hid_codes = []
         hid_scales = []
         for h in range(2):
-            hid_h = sb.tile([P, HALF, 2], F32, name="hid%d" % h, align_bytes=64)
-            codes_h = sb.tile([P, HALF], U32, name="hc%d" % h, align_bytes=64)
-            scales_h = sb.tile([P, HALF], U8, name="hs%d" % h, align_bytes=64)
-            hid.append(hid_h)
+            words_h = sb.tile([P, HALF, 2], F32, name="hid_words%d" % h, align_bytes=64)
+            codes_h = sb.tile([P, HALF], U32, name="hid_codes%d" % h, align_bytes=64)
+            scales_h = sb.tile([P, HALF], U8, name="hid_scales%d" % h, align_bytes=64)
+            hid_words.append(words_h)
             hid_codes.append(codes_h)
             hid_scales.append(scales_h)
 
-        z_halves = {}
-
-        def first_layer_passes(z, j, t0, width, step):
+        def hidden_tile(z, j, t0, width, step):
             for c in range(0, width, step):
-                for g, (w, wz, x, xz, plane) in enumerate(first_layer):
+                for g, (w, w_pass, x, x_pass, x_at) in enumerate(first_layer):
                     nc.tensor.matmul_mx(
                         out=z[:, c : c + step],
-                        lhsT=w[:, wz, 2 * P * j : 2 * P * (j + 1)].bitcast(E2M1X4),
-                        lhsT_scale=w_scale[j][g],
-                        rhs=x[:, xz, t0 + c : t0 + c + step].bitcast(E4M3X4),
-                        rhs_scale=planes1[:, plane * COLS + t0 + c : plane * COLS + t0 + c + step],
+                        lhsT=w[:, w_pass, 2 * P * j : 2 * P * (j + 1)].bitcast(E2M1X4),
+                        lhsT_scale=w_scales[j][g],
+                        rhs=x[:, x_pass, t0 + c : t0 + c + step].bitcast(E4M3X4),
+                        rhs_scale=planes1[:, x_at * COLS + t0 + c : x_at * COLS + t0 + c + step],
                         start=(c == 0 and g == 0),
-                        stop=(c + step == width and g == 2),
+                        stop=(c + step == width and g == n_first - 1),
                     )
             n_tanh = min(width, T - 1 - t0)
-            nc.scalar.activation(out=th[j][:, PAD + t0 : PAD + t0 + n_tanh], in_=z[:, 0:n_tanh], func=ACT.Tanh)
+            nc.scalar.activation(out=tanh_z[j][:, PAD + t0 : PAD + t0 + n_tanh], in_=z[:, 0:n_tanh], func=ACT.Tanh)
 
-        def product(j, h):
+        z_halves = {}
+        for j in range(WHOLE_TILES):
+            z = ps.tile([P, T], F32, name="z%d" % j, tag="z%d" % j)
+            hidden_tile(z, j, 0, T, T)
+            for h in range(2):
+                z_halves[j, h] = z[:, h * HALF : (h + 1) * HALF]
+        for h in range(2):
+            for j in range(WHOLE_TILES, PACK):
+                z = ps.tile([P, HALF], F32, name="z%d%d" % (j, h), tag="z%d%d" % (j, h))
+                hidden_tile(z, j, h * HALF, HALF, P)
+                z_halves[j, h] = z[:]
+
+        others = range(1, PACK)
+        for j, h in [(0, 0), (0, 1)] + [(j, 0) for j in others] + [(j, 1) for j in others]:
             t0 = h * HALF
             nc.vector.scalar_tensor_tensor(
                 out=pairs[h][:, j // 2, :, j % 2],
                 in0=z_halves[j, h],
                 scalar=us_sb[:, j : j + 1],
-                in1=th[j][:, PAD - 1 + t0 : PAD - 1 + t0 + HALF],
+                in1=tanh_z[j][:, PAD - 1 + t0 : PAD - 1 + t0 + HALF],
                 op0=ALU.mult,
                 op1=ALU.mult,
             )
-
-        def merge(h):
+        for h in range(2):
             pair_words = pairs[h][:].rearrange("p u t e -> p u (t e)").bitcast(F32)
-            nc.scalar.copy(out=hid[h][:], in_=pair_words.rearrange("p u t -> p t u"))
-
-        def quantise(h):
+            nc.scalar.copy(out=hid_words[h][:], in_=pair_words.rearrange("p u t -> p t u"))
             nc.vector.quantize_mx(
                 out=hid_codes[h][:].bitcast(E4M3X4),
                 scales=hid_scales[h][:],
-                in_=hid[h][:].rearrange("p t u -> p (t u)").bitcast(BF16),
+                in_=hid_words[h][:].rearrange("p t u -> p (t u)").bitcast(BF16),
             )
-
-        for j in range(2):
-            z = ps.tile([P, T], F32, name="z%d" % j, tag="z%d" % j)
-            first_layer_passes(z, j, 0, T, T)
-            for h in range(2):
-                z_halves[j, h] = z[:, h * HALF : (h + 1) * HALF]
-        for h in range(2):
-            for j in range(2, PACK):
-                z = ps.tile([P, HALF], F32, name="z%d%d" % (j, h), tag="z%d%d" % (j, h))
-                first_layer_passes(z, j, h * HALF, HALF, P)
-                z_halves[j, h] = z[:]
-
-        for j, h in ((0, 0), (0, 1), (1, 0), (2, 0), (3, 0), (1, 1), (2, 1), (3, 1)):
-            product(j, h)
-        for h in range(2):
-            merge(h)
-            quantise(h)
 
         for tag in ("z0", "z20", "z30", "z1", "z21", "z31"):
             acc_i = ps.tile([P, HALF], F32, name="acc_" + tag, tag=tag)
@@ -221,43 +221,47 @@ def tile_mix_hidden_pairs_multiplied_kernel(
 
         def skip_passes(h, i):
             for g in range(2):
-                for c in range(2):
-                    t0 = h * HALF + c * P
+                for c in range(0, HALF, P):
+                    t0 = h * HALF + c
                     nc.tensor.matmul_mx(
-                        out=acc[4 * h + i][:, c * P : (c + 1) * P],
+                        out=acc[N_TILES * h + i][:, c : c + P],
                         lhsT=wy[:, g, 2 * P * i : 2 * P * (i + 1)].bitcast(E2M1X4),
-                        lhsT_scale=planes2[:, g * COLS + P * i : g * COLS + P * (i + 1)],
+                        lhsT_scale=planes2[:, (WY_AT + g) * COLS + P * i : (WY_AT + g) * COLS + P * (i + 1)],
                         rhs=xt[:, g, t0 : t0 + P].bitcast(E4M3X4),
-                        rhs_scale=planes1[:, (3 + g) * COLS + t0 : (3 + g) * COLS + t0 + P],
+                        rhs_scale=planes1[:, (XT_AT + g) * COLS + t0 : (XT_AT + g) * COLS + t0 + P],
                         start=(c == 0 and g == 0),
                         stop=False,
                     )
 
         def hidden_pass(h, i):
             nc.tensor.matmul_mx(
-                out=acc[4 * h + i][:],
+                out=acc[N_TILES * h + i][:],
                 lhsT=wb[:, 0, P * i : P * (i + 1)].bitcast(E4M3X4),
-                lhsT_scale=planes2[:, 2 * COLS + P * i : 2 * COLS + P * (i + 1)],
+                lhsT_scale=planes2[:, WB_AT * COLS + P * i : WB_AT * COLS + P * (i + 1)],
                 rhs=hid_codes[h][:].bitcast(E4M3X4),
                 rhs_scale=hid_scales[h][:],
                 start=False,
                 stop=True,
             )
 
-        for i in range(4):
+        last = N_TILES - 1
+        for i in range(N_TILES):
             skip_passes(0, i)
-        for i in range(3):
-            skip_passes(1, i)
-        for i in range(4):
+        skip_passes(1, 0)
+        for i in range(N_TILES):
             hidden_pass(0, i)
-        skip_passes(1, 3)
-        for i in range(4):
+        for i in range(1, last):
+            skip_passes(1, i)
+        for i in range(last):
             hidden_pass(1, i)
+        skip_passes(1, last)
+        hidden_pass(1, last)
+
         for h in range(2):
-            for i in range(4):
+            for i in range(N_TILES):
                 res = sb.tile([P, HALF], F32, name="res%d%d" % (h, i))
                 if h == 1 and i % 2 == 0:
-                    nc.vector.tensor_copy(out=res[:], in_=acc[4 * h + i][:])
+                    nc.vector.tensor_copy(out=res[:], in_=acc[N_TILES * h + i][:])
                 else:
-                    nc.scalar.copy(out=res[:], in_=acc[4 * h + i][:])
+                    nc.scalar.copy(out=res[:], in_=acc[N_TILES * h + i][:])
                 nc.sync.dma_start(out=out[P * i : P * (i + 1), h * HALF : (h + 1) * HALF], in_=res[:])

from contextlib import ExitStack

import concourse.mybir as mybir

K, L, T, R, N = 1024, 512, 512, 512, 512
FLOPS = 2 * T * (K * R + L * R + R * N + K * N)

F32 = mybir.dt.float32
BF16 = mybir.dt.bfloat16
I32 = mybir.dt.int32
U32 = mybir.dt.uint32
U16 = mybir.dt.uint16
U8 = mybir.dt.uint8
E4M3X4 = mybir.dt.float8_e4m3fn_x4
E2M1X4 = mybir.dt.float4_e2m1fn_x4
ACT = mybir.ActivationFunctionType
ALU = mybir.AluOpType

P = 128
PACK = 4
COLS = 512
HALF = T // 2
N_TILES = N // P
SCALE_ROWS = 16
QUADRANT = 32
STAGE_ROW = 16
PAD = 4
WHOLE_TILES = 2
WARM_AT_START = 18
WARM_AFTER_XT = 12

WA_AT, WC_AT, XT_AT, XQ_AT, FIRST_PASSES = 0, 2, 3, 5, 6
WY_AT, WB_AT, SECOND_PASSES = 0, 2, 3


def tile_mix_hidden_pairs_multiplied_kernel(
    tc, xt_words, xt_scales, wa_words, wa_scales, xq_words, xq_scales, wc_words, wc_scales,
    us, wb_words, wb_scales, wy_words, wy_scales, out,
):
    nc = tc.nc
    with ExitStack() as ctx:
        sb = ctx.enter_context(tc.tile_pool(name="sb", bufs=1))
        ps = ctx.enter_context(tc.psum_pool(name="ps", bufs=1))
        ctx.enter_context(tc.manual_schedule())

        def stage_scale_rows(engine, stage, at, scales):
            passes = scales.shape[0]
            rows = stage[STAGE_ROW : STAGE_ROW + SCALE_ROWS, at * COLS : (at + passes) * COLS].bitcast(I32)
            engine.dma_start(
                out=rows.rearrange("q (z c) -> q z c", z=passes),
                in_=scales.rearrange("z q c -> q z c").bitcast(I32),
            )

        def spread_scale_rows(engines, planes, stage):
            for s in range(4):
                engines[s % len(engines)].dma_start(
                    out=planes[s:P:QUADRANT, :].bitcast(I32),
                    in_=stage[STAGE_ROW + s : STAGE_ROW + SCALE_ROWS : 4, :].bitcast(I32),
                )

        def load_fp8(engine, name, words):
            codes = sb.tile([P, words.shape[0], COLS], U32, name=name, align_bytes=64)
            engine.dma_start(out=codes[:].bitcast(I32), in_=words.rearrange("z p c b -> p z (c b)").bitcast(I32))
            return codes

        def load_fp4(engine, name, words):
            codes = sb.tile([P, words.shape[0], 2 * COLS], U8, name=name, align_bytes=64)
            engine.dma_start(out=codes[:].bitcast(I32), in_=words.rearrange("z p c -> p z c").bitcast(I32))
            return codes

        stage1 = sb.tile([STAGE_ROW + SCALE_ROWS, FIRST_PASSES * COLS], U8, align_bytes=64)
        planes1 = sb.tile([P, FIRST_PASSES * COLS], U8, align_bytes=64)
        stage2 = sb.tile([STAGE_ROW + SCALE_ROWS, SECOND_PASSES * COLS], U8, align_bytes=64)
        planes2 = sb.tile([P, SECOND_PASSES * COLS], U8, align_bytes=64)
        us_sb = sb.tile([P, PACK], F32)

        stage_scale_rows(nc.sync, stage1, WA_AT, wa_scales)
        stage_scale_rows(nc.scalar, stage1, WC_AT, wc_scales)
        stage_scale_rows(nc.sync, stage1, XT_AT, xt_scales)
        stage_scale_rows(nc.scalar, stage1, XQ_AT, xq_scales)
        stage_scale_rows(nc.sync, stage2, WY_AT, wy_scales)
        stage_scale_rows(nc.scalar, stage2, WB_AT, wb_scales)
        wa = load_fp4(nc.sync, "wa", wa_words)
        xt = load_fp8(nc.scalar, "xt", xt_words)

        zeros = sb.tile([P, PACK * P], BF16, align_bytes=64)
        zero_codes = sb.tile([P, P], U32, align_bytes=64)
        zero_scales = sb.tile([P, P], U8, align_bytes=64)
        nc.vector.memset(zeros[:], 0.0)
        tanh_z = []
        for j in range(PACK):
            tanh_j = sb.tile([P, PAD + T], F32, name="tanh%d" % j, align_bytes=64)
            nc.vector.memset(tanh_j[:, PAD - 1 : PAD], 0.0)
            tanh_z.append(tanh_j)
        nc.vector.quantize_mx(out=zero_codes[:].bitcast(E4M3X4), scales=zero_scales[:], in_=zeros[:])
        nc.vector.memset(planes1[:].bitcast(U32), 0)
        nc.vector.memset(planes2[:].bitcast(U32), 0)

        acc = []
        for i in range(2):
            acc_i = ps.tile([P, HALF], F32, name="acc%d" % i)
            acc.append(acc_i)

        for w in range(WARM_AT_START + WARM_AFTER_XT):
            nc.tensor.matmul_mx(
                out=acc[1][:, 0:P],
                lhsT=(zero_codes[:] if w < WARM_AT_START else xt[:, 0, 0:P]).bitcast(E4M3X4),
                lhsT_scale=zero_scales[:],
                rhs=zero_codes[:].bitcast(E4M3X4),
                rhs_scale=zero_scales[:],
                start=True,
                stop=True,
            )

        spread_scale_rows((nc.sync, nc.scalar), planes1, stage1)
        wc = load_fp4(nc.sync, "wc", wc_words)
        xq = load_fp8(nc.scalar, "xq", xq_words)
        table_warm = sb.tile([P, 1], F32)
        nc.scalar.activation(out=table_warm[:], in_=tanh_z[0][:, PAD - 1 : PAD], func=ACT.Tanh)
        nc.sync.dma_start(out=us_sb[:], in_=us.rearrange("(p j) o -> p (j o)", j=PACK))
        wy = load_fp4(nc.sync, "wy", wy_words)
        spread_scale_rows((nc.sync,), planes2, stage2)
        wb = load_fp8(nc.sync, "wb", wb_words)

        wa_by_tile = sb.tile([P, 2, 2 * COLS], U8, align_bytes=64)
        wc_by_tile = sb.tile([P, 1, 2 * COLS], U8, align_bytes=64)

        def permute_words(dst, src):
            nc.vector.tensor_copy(
                out=dst[:].bitcast(U16).rearrange("p z (j m) -> p z j m", j=PACK),
                in_=src[:].bitcast(U16).rearrange("p z (m j) -> p z j m", j=PACK),
            )

        first_layer = (
            (wa_by_tile, 0, xt, 0, XT_AT),
            (wa_by_tile, 1, xt, 1, XT_AT + 1),
            (wc_by_tile, 0, xq, 0, XQ_AT),
        )
        n_first = len(first_layer)
        weight_planes = planes1[:, 0 : n_first * COLS].rearrange("p (g m j) -> p j g m", g=n_first, j=PACK)

        permute_words(wa_by_tile, wa)
        tile0_scales = []
        for g in range(n_first):
            scales_g = sb.tile([P, P], U8, name="w_scales0%d" % g, align_bytes=64)
            if g == WC_AT:
                permute_words(wc_by_tile, wc)
            nc.vector.tensor_copy(out=scales_g[:], in_=weight_planes[:, 0, g])
            tile0_scales.append(scales_g[:])
        w_scales = [tile0_scales]
        for j in range(1, PACK):
            scales_j = sb.tile([P, n_first, P], U8, name="w_scales%d" % j, align_bytes=64)
            nc.vector.tensor_copy(out=scales_j[:], in_=weight_planes[:, j])
            w_scales.append([scales_j[:, g, :] for g in range(n_first)])

        pairs = []
        for h in range(2):
            pairs_h = sb.tile([P, 2, HALF, 2], BF16, name="pairs%d" % h, align_bytes=64)
            pairs.append(pairs_h)
        hid_words = []
        hid_codes = []
        hid_scales = []
        for h in range(2):
            words_h = sb.tile([P, HALF, 2], F32, name="hid_words%d" % h, align_bytes=64)
            codes_h = sb.tile([P, HALF], U32, name="hid_codes%d" % h, align_bytes=64)
            scales_h = sb.tile([P, HALF], U8, name="hid_scales%d" % h, align_bytes=64)
            hid_words.append(words_h)
            hid_codes.append(codes_h)
            hid_scales.append(scales_h)

        def hidden_tile(z, j, t0, width, step):
            for c in range(0, width, step):
                for g, (w, w_pass, x, x_pass, x_at) in enumerate(first_layer):
                    nc.tensor.matmul_mx(
                        out=z[:, c : c + step],
                        lhsT=w[:, w_pass, 2 * P * j : 2 * P * (j + 1)].bitcast(E2M1X4),
                        lhsT_scale=w_scales[j][g],
                        rhs=x[:, x_pass, t0 + c : t0 + c + step].bitcast(E4M3X4),
                        rhs_scale=planes1[:, x_at * COLS + t0 + c : x_at * COLS + t0 + c + step],
                        start=(c == 0 and g == 0),
                        stop=(c + step == width and g == n_first - 1),
                    )
            n_tanh = min(width, T - 1 - t0)
            nc.scalar.activation(out=tanh_z[j][:, PAD + t0 : PAD + t0 + n_tanh], in_=z[:, 0:n_tanh], func=ACT.Tanh)

        z_halves = {}
        for j in range(WHOLE_TILES):
            z = ps.tile([P, T], F32, name="z%d" % j, tag="z%d" % j)
            hidden_tile(z, j, 0, T, T)
            for h in range(2):
                z_halves[j, h] = z[:, h * HALF : (h + 1) * HALF]
        for h in range(2):
            for j in range(WHOLE_TILES, PACK):
                z = ps.tile([P, HALF], F32, name="z%d%d" % (j, h), tag="z%d%d" % (j, h))
                hidden_tile(z, j, h * HALF, HALF, P)
                z_halves[j, h] = z[:]

        others = range(1, PACK)
        for j, h in [(0, 0), (0, 1)] + [(j, 0) for j in others] + [(j, 1) for j in others]:
            t0 = h * HALF
            nc.vector.scalar_tensor_tensor(
                out=pairs[h][:, j // 2, :, j % 2],
                in0=z_halves[j, h],
                scalar=us_sb[:, j : j + 1],
                in1=tanh_z[j][:, PAD - 1 + t0 : PAD - 1 + t0 + HALF],
                op0=ALU.mult,
                op1=ALU.mult,
            )
        for h in range(2):
            pair_words = pairs[h][:].rearrange("p u t e -> p u (t e)").bitcast(F32)
            nc.scalar.copy(out=hid_words[h][:], in_=pair_words.rearrange("p u t -> p t u"))
            nc.vector.quantize_mx(
                out=hid_codes[h][:].bitcast(E4M3X4),
                scales=hid_scales[h][:],
                in_=hid_words[h][:].rearrange("p t u -> p (t u)").bitcast(BF16),
            )

        for tag in ("z0", "z20", "z30", "z1", "z21", "z31"):
            acc_i = ps.tile([P, HALF], F32, name="acc_" + tag, tag=tag)
            acc.append(acc_i)

        def skip_passes(h, i):
            for g in range(2):
                for c in range(0, HALF, P):
                    t0 = h * HALF + c
                    nc.tensor.matmul_mx(
                        out=acc[N_TILES * h + i][:, c : c + P],
                        lhsT=wy[:, g, 2 * P * i : 2 * P * (i + 1)].bitcast(E2M1X4),
                        lhsT_scale=planes2[:, (WY_AT + g) * COLS + P * i : (WY_AT + g) * COLS + P * (i + 1)],
                        rhs=xt[:, g, t0 : t0 + P].bitcast(E4M3X4),
                        rhs_scale=planes1[:, (XT_AT + g) * COLS + t0 : (XT_AT + g) * COLS + t0 + P],
                        start=(c == 0 and g == 0),
                        stop=False,
                    )

        def hidden_pass(h, i):
            nc.tensor.matmul_mx(
                out=acc[N_TILES * h + i][:],
                lhsT=wb[:, 0, P * i : P * (i + 1)].bitcast(E4M3X4),
                lhsT_scale=planes2[:, WB_AT * COLS + P * i : WB_AT * COLS + P * (i + 1)],
                rhs=hid_codes[h][:].bitcast(E4M3X4),
                rhs_scale=hid_scales[h][:],
                start=False,
                stop=True,
            )

        last = N_TILES - 1
        for i in range(N_TILES):
            skip_passes(0, i)
        skip_passes(1, 0)
        for i in range(N_TILES):
            hidden_pass(0, i)
        for i in range(1, last):
            skip_passes(1, i)
        for i in range(last):
            hidden_pass(1, i)
        skip_passes(1, last)
        hidden_pass(1, last)

        for h in range(2):
            for i in range(N_TILES):
                res = sb.tile([P, HALF], F32, name="res%d%d" % (h, i))
                if h == 1 and i % 2 == 0:
                    nc.vector.tensor_copy(out=res[:], in_=acc[N_TILES * h + i][:])
                else:
                    nc.scalar.copy(out=res[:], in_=acc[N_TILES * h + i][:])
                nc.sync.dma_start(out=out[P * i : P * (i + 1), h * HALF : (h + 1) * HALF], in_=res[:])
